import numpy as np
import ml_dtypes


def mxq(x, axis, fmt="e4m3"):
    dtype, down = {"e4m3": (ml_dtypes.float8_e4m3fn, 7), "e5m2": (ml_dtypes.float8_e5m2, 14)}[fmt]
    v = np.moveaxis(np.asarray(x, np.float32).astype(ml_dtypes.bfloat16).astype(np.float64), axis, -1)
    blocks = v.reshape(v.shape[:-1] + (-1, 32))
    amax = np.abs(blocks).max(-1, keepdims=True)
    byte = np.maximum(np.where(amax > 0, np.frexp(amax)[1] - 1 + 127, 0) - down, 1)
    scale = np.exp2(byte - 127.0)
    codes = (blocks / scale).astype(np.float32).astype(dtype).astype(np.float64)
    return np.moveaxis((codes * scale).reshape(v.shape), -1, axis)


WIDE = False


def mx_kscale(k):
    if not WIDE:
        return np.ones(k)
    levels = np.array([10, -10, 5, -5, 0])
    if k % 512:
        return np.exp2(np.random.permutation(np.resize(levels, k // 32))).repeat(32)
    a = np.empty((k // 512, 16))
    for p in range(k // 512):
        a[p, :8] = np.random.permutation(np.resize(levels, 8))
        for g in range(8):
            far = levels[np.abs(levels - a[p, g]) >= 10]
            a[p, g + 8] = far[np.random.randint(len(far))]
    return np.exp2(a.ravel()).repeat(32)


def f64(x):
    return np.asarray(x).astype(np.float64)


def striped8(idx):
    return np.concatenate([v.reshape(-1, 16).T for v in idx]).astype(np.uint16)


def unstriped8(offs):
    return np.stack([offs[16 * g:16 * g + 16].T.reshape(-1) for g in range(8)]).astype(np.int64)


E2M1 = np.array([0.0, 0.5, 1.0, 1.5, 2.0, 3.0, 4.0, 6.0, -0.0, -0.5, -1.0, -1.5, -2.0, -3.0, -4.0, -6.0])


def pack_weight(w, fmt):
    k, n = w.shape
    w = f64(np.asarray(w, np.float32).astype(ml_dtypes.bfloat16)).reshape(k // 32, 32, n)
    amax = np.abs(w).max(1)
    if fmt == "e4m3":
        byte = np.frexp(amax)[1] - 1 + 127 - 7
    else:
        mant, ex = np.frexp(amax / 6.0)
        byte = np.where(mant > 0.5, ex, ex - 1) + 127
    byte = np.clip(np.where(amax > 0, byte, 1), 1, 254)
    scaled = (w * np.exp2(127.0 - byte)[:, None, :]).reshape(k, n).astype(np.float32)
    by_word = np.ascontiguousarray(scaled.reshape(k // 512, 128, 4, n).transpose(0, 1, 3, 2))
    if fmt == "e4m3":
        words = by_word.astype(ml_dtypes.float8_e4m3fn).view(np.uint8)
    else:
        c = by_word.astype(ml_dtypes.float4_e2m1fn).view(np.uint8) & 0xF
        words = (c[..., 0::2] | (c[..., 1::2] << 4)).reshape(k // 512, 128, 2 * n)
    return np.ascontiguousarray(words), np.ascontiguousarray(byte.astype(np.uint8).reshape(k // 512, 16, n))


def unpack_weight(words, scales, fmt):
    g, _, n = scales.shape
    words = np.ascontiguousarray(words).reshape(g, 128, n, -1)
    if fmt == "e4m3":
        vals = words.view(ml_dtypes.float8_e4m3fn).astype(np.float64)
    else:
        nib = np.empty((g, 128, n, 4), np.uint8)
        nib[..., 0::2] = words & 0xF
        nib[..., 1::2] = words >> 4
        vals = E2M1[nib]
    vals = vals * np.repeat(np.exp2(scales.astype(np.float64) - 127.0), 8, axis=1)[..., None]
    return vals.transpose(0, 1, 3, 2).reshape(g * 512, n)


def silu(v):
    return v / (1.0 + np.exp(-np.maximum(v, -700.0)))


K, M, T, S = 2048, 512, 4096, 2048


def setup_inputs():
    n = np.random.standard_normal
    s = mx_kscale(K)[:, None]
    p_w = pack_weight(n((K, M)) / np.sqrt(K) / s, "e2m1")
    return {
        "x": (n((K, S)) * s).astype(np.float32),
        "w_words": p_w[0],
        "w_scales": p_w[1],
        "b": (0.3 * n(512)).astype(np.float32),
        "wgo": np.repeat(np.random.uniform(0.5, 2.0, (8, S)), 16, axis=0).astype(np.float32),
        "offs": striped8(np.stack([np.random.permutation(T)[:S] for _ in range(8)])),
    }


def reference(x, w_words, w_scales, b, wgo, offs):
    x_ = mxq(f64(x), 0, "e4m3")
    w_ = unpack_weight(w_words, w_scales, "e2m1")
    y = w_.T @ x_
    place = unstriped8(offs)[np.arange(M) % 128 // 16]
    out = np.zeros((M, T))
    out[np.arange(M)[:, None], place] = f64(wgo)[np.arange(M) % 128] * (silu(y + f64(b)[:, None]))
    return out

@@ -1,0 +1,136 @@
+from contextlib import ExitStack
+
+import concourse.mybir as mybir
+
+F32 = mybir.dt.float32
+BF16 = mybir.dt.bfloat16
+I32 = mybir.dt.int32
+U32 = mybir.dt.uint32
+U16 = mybir.dt.uint16
+U8 = mybir.dt.uint8
+E4M3 = mybir.dt.float8_e4m3fn_x4
+E2M1 = mybir.dt.float4_e2m1fn_x4
+SILU = mybir.ActivationFunctionType.Silu
+MULT = mybir.AluOpType.mult
+
+K, M, T, S = 2048, 512, 4096, 2048
+P = 128
+PASSES = K // 512
+BLOCKS = M // P
+HALF = S // 2
+BANK = 512
+FLOPS = 2 * K * M * S
+
+FULL = [(0, 1024, 640)]
+LAST0 = [(0, 512, 256), (512, 512, 192)]
+CHUNKS = [[FULL, FULL, FULL, LAST0], [[(0, 512, 512), (512, 512, 512)], [(0, 1024, 1024)], [(0, 1024, 1024)], [(0, 512, 512), (512, 512, 512)]]]
+
+
+def tile_list_hscat_silu_kernel(tc, x, w_words, w_scales, b, wgo, offs, out):
+    nc = tc.nc
+    with ExitStack() as ctx:
+        keep = ctx.enter_context(tc.tile_pool(name="keep", bufs=1))
+        stage = ctx.enter_context(tc.tile_pool(name="stage", bufs=6))
+        group = ctx.enter_context(tc.tile_pool(name="group", bufs=3))
+        quant = ctx.enter_context(tc.tile_pool(name="quant", bufs=5))
+        result = ctx.enter_context(tc.tile_pool(name="result", bufs=3))
+        psum = ctx.enter_context(tc.psum_pool(name="psum", bufs=1))
+
+        offs_sb = keep.tile([P, S // 16], U16, name="offs_sb")
+        wgo_sb = keep.tile([P, S], F32, name="wgo_sb")
+        w_sb = keep.tile([P, PASSES, 2 * M], U8, name="w_sb", align_bytes=64)
+        ws_sb = keep.tile([P, PASSES, M], U8, name="ws_sb", align_bytes=64)
+        b_sb = keep.tile([P, BLOCKS], F32, name="b_sb")
+        tiny = keep.tile([P, 8], F32, name="tiny")
+        windows = [keep.tile([P, T], F32, name=f"window{m}") for m in range(2)]
+
+        raw = {}
+
+        def load(h, a):
+            for c0, cols, scalar_cols in CHUNKS[h][a]:
+                t = stage.tile([P, 4, cols], F32, name="raw", tag="stage")
+                lo = h * HALF + c0
+                nc.sync.dma_start(t[:], x[512 * a : 512 * a + 512, lo : lo + cols].rearrange("(p i) j -> p i j", i=4))
+                raw[h, a, c0] = t
+
+        load(0, 0)
+        nc.vector.memset(tiny[:], 0.0)
+        nc.vector.memset(ws_sb[:].bitcast(I32), 0)
+        nc.scalar.activation(tiny[:, 0:1], tiny[:, 1:2], SILU)
+        nc.scalar.dma_start(w_sb[:].bitcast(I32), w_words.rearrange("a p c -> p a c").bitcast(I32))
+        for q in range(4):
+            nc.scalar.dma_start(ws_sb[32 * q : 32 * q + 4, :, :].bitcast(I32), w_scales[:, 4 * q : 4 * q + 4, :].rearrange("a q n -> q a n").bitcast(I32))
+        with nc.allow_non_contiguous_dma(reason="512 bias values, one to a partition and block"):
+            nc.scalar.dma_start(b_sb[:], b.rearrange("(m p) -> p m", p=P))
+        load(0, 1)
+        nc.vector.memset(windows[0][:], 0.0)
+        nc.gpsimd.memset(windows[1][:], 0.0)
+        load(0, 2)
+        load(0, 3)
+        nc.sync.dma_start(offs_sb[:], offs)
+        nc.sync.dma_start(wgo_sb[:, 0:HALF], wgo[:, 0:HALF])
+
+        def interleave(dst, src, engine):
+            engine(dst.rearrange("p (c i) t -> p c t i", i=4), src.rearrange("p t (c i) -> p c t i", i=4))
+
+        banks = {}
+
+        def contract(h, a):
+            codes = quant.tile([P, HALF], U32, name="codes", align_bytes=64)
+            scales = quant.tile([P, HALF], U8, name="scales", align_bytes=64)
+            for c0, cols, scalar_cols in CHUNKS[h][a]:
+                grouped = group.tile([P, cols, 4], BF16, name="grouped", align_bytes=64)
+                src = raw[h, a, c0]
+                if scalar_cols > 0:
+                    interleave(grouped[:, 0:scalar_cols, :], src[:, :, 0:scalar_cols], nc.scalar.copy)
+                if scalar_cols < cols:
+                    interleave(grouped[:, scalar_cols:cols, :], src[:, :, scalar_cols:cols], nc.vector.tensor_copy)
+                nc.vector.quantize_mx(
+                    out=codes[:, c0 : c0 + cols].bitcast(E4M3),
+                    scales=scales[:, c0 : c0 + cols],
+                    in_=grouped[:].rearrange("p c t -> p (c t)"),
+                )
+                for u in range(0, cols, BANK):
+                    lo = c0 + u
+                    n = lo // BANK
+                    for m in range(BLOCKS):
+                        if a == 0:
+                            banks[h, m, n] = psum.tile([P, BANK], F32, name=f"bank{m}{n}")
+                        nc.tensor.matmul_mx(
+                            out=banks[h, m, n][:],
+                            lhsT=w_sb[:, a, 2 * P * m : 2 * P * (m + 1)].bitcast(E2M1),
+                            lhsT_scale=ws_sb[:, a, P * m : P * (m + 1)],
+                            rhs=codes[:, lo : lo + BANK].bitcast(E4M3),
+                            rhs_scale=scales[:, lo : lo + BANK],
+                            start=(a == 0),
+                            stop=(a == PASSES - 1),
+                        )
+
+        def place(h, m):
+            y = result.tile([P, HALF], F32, name="y")
+            for n in range(HALF // BANK):
+                nc.scalar.activation(y[:, n * BANK : (n + 1) * BANK], banks[h, m, n][:], SILU, bias=b_sb[:, m : m + 1])
+            nc.vector.tensor_tensor(
+                windows[m][:].indirect(offs_sb[:, h * HALF // 16 : (h + 1) * HALF // 16]),
+                y[:],
+                wgo_sb[:, h * HALF : (h + 1) * HALF],
+                MULT,
+            )
+
+        for a in range(PASSES):
+            contract(0, a)
+        load(1, 0)
+        load(1, 1)
+        nc.sync.dma_start(wgo_sb[:, HALF:S], wgo[:, HALF:S])
+        load(1, 2)
+        load(1, 3)
+        for m in range(2, BLOCKS):
+            window = stage.tile([P, T], F32, name="window", tag="stage")
+            nc.gpsimd.memset(window[:], 0.0)
+            windows.append(window)
+        for m in range(BLOCKS):
+            place(0, m)
+            contract(1, m)
+        for m in range(BLOCKS):
+            place(1, m)
+            nc.sync.dma_start(out[P * m : P * (m + 1), :], windows[m][:])

@@ -21,9 +21,10 @@ HALF = S // 2
 BANK = 512
 FLOPS = 2 * K * M * S
 
-FULL = [(0, 1024, 640)]
-LAST0 = [(0, 512, 256), (512, 512, 192)]
-CHUNKS = [[FULL, FULL, FULL, LAST0], [[(0, 512, 512), (512, 512, 512)], [(0, 1024, 1024)], [(0, 1024, 1024)], [(0, 512, 512), (512, 512, 512)]]]
+CHUNKS = [
+    [[(0, 1024, 640)], [(0, 1024, 640)], [(0, 1024, 640)], [(0, 512, 256), (512, 256, 128), (768, 256, 96)]],
+    [[(0, 512, 512), (512, 512, 512)], [(0, 1024, 1024)], [(0, 1024, 1024)], [(0, 512, 512), (512, 512, 64)]],
+]
 
 
 def tile_list_hscat_silu_kernel(tc, x, w_words, w_scales, b, wgo, offs, out):
@@ -38,13 +39,18 @@ def tile_list_hscat_silu_kernel(tc, x, w_words, w_scales, b, wgo, offs, out):
 
         offs_sb = keep.tile([P, S // 16], U16, name="offs_sb")
         wgo_sb = keep.tile([P, S], F32, name="wgo_sb")
-        w_sb = keep.tile([P, PASSES, 2 * M], U8, name="w_sb", align_bytes=64)
+        w0_sb = keep.tile([P, PASSES, 2 * P], U8, name="w0_sb", align_bytes=64)
+        w1_sb = keep.tile([P, PASSES, 2 * (M - P)], U8, name="w1_sb", align_bytes=64)
         ws_sb = keep.tile([P, PASSES, M], U8, name="ws_sb", align_bytes=64)
         b_sb = keep.tile([P, BLOCKS], F32, name="b_sb")
         tiny = keep.tile([P, 8], F32, name="tiny")
-        windows = [keep.tile([P, T], F32, name=f"window{m}") for m in range(2)]
+        windows = [keep.tile([P, T], F32, name=f"window{m}") for m in range(3)]
+        w_view = w_words.rearrange("a p c -> p a c")
 
         raw = {}
+        banks = {}
+        codes = {}
+        scales = {}
 
         def load(h, a):
             for c0, cols, scalar_cols in CHUNKS[h][a]:
@@ -53,31 +59,15 @@ def tile_list_hscat_silu_kernel(tc, x, w_words, w_scales, b, wgo, offs, out):
                 nc.sync.dma_start(t[:], x[512 * a : 512 * a + 512, lo : lo + cols].rearrange("(p i) j -> p i j", i=4))
                 raw[h, a, c0] = t
 
-        load(0, 0)
-        nc.vector.memset(tiny[:], 0.0)
-        nc.vector.memset(ws_sb[:].bitcast(I32), 0)
-        nc.scalar.activation(tiny[:, 0:1], tiny[:, 1:2], SILU)
-        nc.scalar.dma_start(w_sb[:].bitcast(I32), w_words.rearrange("a p c -> p a c").bitcast(I32))
-        for q in range(4):
-            nc.scalar.dma_start(ws_sb[32 * q : 32 * q + 4, :, :].bitcast(I32), w_scales[:, 4 * q : 4 * q + 4, :].rearrange("a q n -> q a n").bitcast(I32))
-        with nc.allow_non_contiguous_dma(reason="512 bias values, one to a partition and block"):
-            nc.scalar.dma_start(b_sb[:], b.rearrange("(m p) -> p m", p=P))
-        load(0, 1)
-        nc.vector.memset(windows[0][:], 0.0)
-        nc.gpsimd.memset(windows[1][:], 0.0)
-        load(0, 2)
-        load(0, 3)
-        nc.sync.dma_start(offs_sb[:], offs)
-        nc.sync.dma_start(wgo_sb[:, 0:HALF], wgo[:, 0:HALF])
+        def clear(engine, m, lo, hi):
+            engine.memset(windows[m][:, lo:hi], 0.0)
 
         def interleave(dst, src, engine):
             engine(dst.rearrange("p (c i) t -> p c t i", i=4), src.rearrange("p t (c i) -> p c t i", i=4))
 
-        banks = {}
-
-        def contract(h, a):
-            codes = quant.tile([P, HALF], U32, name="codes", align_bytes=64)
-            scales = quant.tile([P, HALF], U8, name="scales", align_bytes=64)
+        def quantize(h, a):
+            codes[h, a] = quant.tile([P, HALF], U32, name="codes", align_bytes=64)
+            scales[h, a] = quant.tile([P, HALF], U8, name="scales", align_bytes=64)
             for c0, cols, scalar_cols in CHUNKS[h][a]:
                 grouped = group.tile([P, cols, 4], BF16, name="grouped", align_bytes=64)
                 src = raw[h, a, c0]
@@ -86,25 +76,25 @@ def tile_list_hscat_silu_kernel(tc, x, w_words, w_scales, b, wgo, offs, out):
                 if scalar_cols < cols:
                     interleave(grouped[:, scalar_cols:cols, :], src[:, :, scalar_cols:cols], nc.vector.tensor_copy)
                 nc.vector.quantize_mx(
-                    out=codes[:, c0 : c0 + cols].bitcast(E4M3),
-                    scales=scales[:, c0 : c0 + cols],
+                    out=codes[h, a][:, c0 : c0 + cols].bitcast(E4M3),
+                    scales=scales[h, a][:, c0 : c0 + cols],
                     in_=grouped[:].rearrange("p c t -> p (c t)"),
                 )
-                for u in range(0, cols, BANK):
-                    lo = c0 + u
-                    n = lo // BANK
-                    for m in range(BLOCKS):
-                        if a == 0:
-                            banks[h, m, n] = psum.tile([P, BANK], F32, name=f"bank{m}{n}")
-                        nc.tensor.matmul_mx(
-                            out=banks[h, m, n][:],
-                            lhsT=w_sb[:, a, 2 * P * m : 2 * P * (m + 1)].bitcast(E2M1),
-                            lhsT_scale=ws_sb[:, a, P * m : P * (m + 1)],
-                            rhs=codes[:, lo : lo + BANK].bitcast(E4M3),
-                            rhs_scale=scales[:, lo : lo + BANK],
-                            start=(a == 0),
-                            stop=(a == PASSES - 1),
-                        )
+
+        def multiply(h, a, m):
+            words = w0_sb[:, a, :] if m == 0 else w1_sb[:, a, 2 * P * (m - 1) : 2 * P * m]
+            for n in range(HALF // BANK):
+                if a == 0:
+                    banks[h, m, n] = psum.tile([P, BANK], F32, name=f"bank{m}{n}")
+                nc.tensor.matmul_mx(
+                    out=banks[h, m, n][:],
+                    lhsT=words.bitcast(E2M1),
+                    lhsT_scale=ws_sb[:, a, P * m : P * (m + 1)],
+                    rhs=codes[h, a][:, n * BANK : (n + 1) * BANK].bitcast(E4M3),
+                    rhs_scale=scales[h, a][:, n * BANK : (n + 1) * BANK],
+                    start=(a == 0),
+                    stop=(a == PASSES - 1),
+                )
 
         def place(h, m):
             y = result.tile([P, HALF], F32, name="y")
@@ -117,20 +107,53 @@ def tile_list_hscat_silu_kernel(tc, x, w_words, w_scales, b, wgo, offs, out):
                 MULT,
             )
 
+        load(0, 0)
+        nc.vector.memset(tiny[:], 0.0)
+        nc.vector.memset(ws_sb[:].bitcast(I32), 0)
+        nc.scalar.activation(tiny[:, 0:1], tiny[:, 1:2], SILU)
+        nc.scalar.dma_start(w0_sb[:].bitcast(I32), w_view[:, :, 0 : 2 * P].bitcast(I32))
+        for q in range(4):
+            nc.scalar.dma_start(ws_sb[32 * q : 32 * q + 4, :, :].bitcast(I32), w_scales[:, 4 * q : 4 * q + 4, :].rearrange("a q n -> q a n").bitcast(I32))
+        with nc.allow_non_contiguous_dma(reason="512 bias values, one to a partition and block"):
+            nc.scalar.dma_start(b_sb[:], b.rearrange("(m p) -> p m", p=P))
+        for a in range(1, PASSES):
+            load(0, a)
+        nc.sync.dma_start(offs_sb[:], offs)
+        nc.sync.dma_start(wgo_sb[:, 0:HALF], wgo[:, 0:HALF])
+        nc.sync.dma_start(w1_sb[:].bitcast(I32), w_view[:, :, 2 * P : 2 * M].bitcast(I32))
+        clear(nc.vector, 0, 0, 2048)
+        for lo in range(0, T, 1024):
+            clear(nc.gpsimd, 2, lo, lo + 1024)
+
         for a in range(PASSES):
-            contract(0, a)
+            quantize(0, a)
+            multiply(0, a, 0)
+            if a == 0:
+                clear(nc.vector, 0, 2048, 3072)
+                clear(nc.vector, 0, 3072, 4096)
+            elif a < 3:
+                clear(nc.vector, 1, 2048 * (a - 1), 2048 * (a - 1) + 1024)
+                clear(nc.vector, 1, 2048 * (a - 1) + 1024, 2048 * a)
         load(1, 0)
         load(1, 1)
         nc.sync.dma_start(wgo_sb[:, HALF:S], wgo[:, HALF:S])
         load(1, 2)
         load(1, 3)
-        for m in range(2, BLOCKS):
-            window = stage.tile([P, T], F32, name="window", tag="stage")
-            nc.gpsimd.memset(window[:], 0.0)
-            windows.append(window)
+        window = stage.tile([P, T], F32, name="window", tag="stage")
+        windows.append(window)
+        for lo in range(0, T, 512):
+            clear(nc.gpsimd, 3, lo, lo + 512)
         for m in range(BLOCKS):
+            if m > 0:
+                for a in range(PASSES):
+                    multiply(0, a, m)
+            if m == BLOCKS - 1:
+                quantize(1, m)
             place(0, m)
-            contract(1, m)
+            if m < BLOCKS - 1:
+                quantize(1, m)
         for m in range(BLOCKS):
+            for a in range(PASSES):
+                multiply(1, a, m)
             place(1, m)
             nc.sync.dma_start(out[P * m : P * (m + 1), :], windows[m][:])

from contextlib import ExitStack

import concourse.mybir as mybir

F32 = mybir.dt.float32
BF16 = mybir.dt.bfloat16
I32 = mybir.dt.int32
U32 = mybir.dt.uint32
U16 = mybir.dt.uint16
U8 = mybir.dt.uint8
E4M3 = mybir.dt.float8_e4m3fn_x4
E2M1 = mybir.dt.float4_e2m1fn_x4
SILU = mybir.ActivationFunctionType.Silu
MULT = mybir.AluOpType.mult

K, M, T, S = 2048, 512, 4096, 2048
P = 128
PASSES = K // 512
BLOCKS = M // P
HALF = S // 2
BANK = 512
FLOPS = 2 * K * M * S

CHUNKS = [
    [[(0, 1024, 640)], [(0, 1024, 640)], [(0, 1024, 640)], [(0, 512, 256), (512, 256, 128), (768, 256, 96)]],
    [[(0, 512, 512), (512, 512, 512)], [(0, 1024, 1024)], [(0, 1024, 1024)], [(0, 512, 512), (512, 512, 64)]],
]


def tile_list_hscat_silu_kernel(tc, x, w_words, w_scales, b, wgo, offs, out):
    nc = tc.nc
    with ExitStack() as ctx:
        keep = ctx.enter_context(tc.tile_pool(name="keep", bufs=1))
        stage = ctx.enter_context(tc.tile_pool(name="stage", bufs=6))
        group = ctx.enter_context(tc.tile_pool(name="group", bufs=3))
        quant = ctx.enter_context(tc.tile_pool(name="quant", bufs=5))
        result = ctx.enter_context(tc.tile_pool(name="result", bufs=3))
        psum = ctx.enter_context(tc.psum_pool(name="psum", bufs=1))

        offs_sb = keep.tile([P, S // 16], U16, name="offs_sb")
        wgo_sb = keep.tile([P, S], F32, name="wgo_sb")
        w0_sb = keep.tile([P, PASSES, 2 * P], U8, name="w0_sb", align_bytes=64)
        w1_sb = keep.tile([P, PASSES, 2 * (M - P)], U8, name="w1_sb", align_bytes=64)
        ws_sb = keep.tile([P, PASSES, M], U8, name="ws_sb", align_bytes=64)
        b_sb = keep.tile([P, BLOCKS], F32, name="b_sb")
        tiny = keep.tile([P, 8], F32, name="tiny")
        windows = [keep.tile([P, T], F32, name=f"window{m}") for m in range(3)]
        w_view = w_words.rearrange("a p c -> p a c")

        raw = {}
        banks = {}
        codes = {}
        scales = {}

        def load(h, a):
            for c0, cols, scalar_cols in CHUNKS[h][a]:
                t = stage.tile([P, 4, cols], F32, name="raw", tag="stage")
                lo = h * HALF + c0
                nc.sync.dma_start(t[:], x[512 * a : 512 * a + 512, lo : lo + cols].rearrange("(p i) j -> p i j", i=4))
                raw[h, a, c0] = t

        def clear(engine, m, lo, hi):
            engine.memset(windows[m][:, lo:hi], 0.0)

        def interleave(dst, src, engine):
            engine(dst.rearrange("p (c i) t -> p c t i", i=4), src.rearrange("p t (c i) -> p c t i", i=4))

        def quantize(h, a):
            codes[h, a] = quant.tile([P, HALF], U32, name="codes", align_bytes=64)
            scales[h, a] = quant.tile([P, HALF], U8, name="scales", align_bytes=64)
            for c0, cols, scalar_cols in CHUNKS[h][a]:
                grouped = group.tile([P, cols, 4], BF16, name="grouped", align_bytes=64)
                src = raw[h, a, c0]
                if scalar_cols > 0:
                    interleave(grouped[:, 0:scalar_cols, :], src[:, :, 0:scalar_cols], nc.scalar.copy)
                if scalar_cols < cols:
                    interleave(grouped[:, scalar_cols:cols, :], src[:, :, scalar_cols:cols], nc.vector.tensor_copy)
                nc.vector.quantize_mx(
                    out=codes[h, a][:, c0 : c0 + cols].bitcast(E4M3),
                    scales=scales[h, a][:, c0 : c0 + cols],
                    in_=grouped[:].rearrange("p c t -> p (c t)"),
                )

        def multiply(h, a, m):
            words = w0_sb[:, a, :] if m == 0 else w1_sb[:, a, 2 * P * (m - 1) : 2 * P * m]
            for n in range(HALF // BANK):
                if a == 0:
                    banks[h, m, n] = psum.tile([P, BANK], F32, name=f"bank{m}{n}")
                nc.tensor.matmul_mx(
                    out=banks[h, m, n][:],
                    lhsT=words.bitcast(E2M1),
                    lhsT_scale=ws_sb[:, a, P * m : P * (m + 1)],
                    rhs=codes[h, a][:, n * BANK : (n + 1) * BANK].bitcast(E4M3),
                    rhs_scale=scales[h, a][:, n * BANK : (n + 1) * BANK],
                    start=(a == 0),
                    stop=(a == PASSES - 1),
                )

        def place(h, m):
            y = result.tile([P, HALF], F32, name="y")
            for n in range(HALF // BANK):
                nc.scalar.activation(y[:, n * BANK : (n + 1) * BANK], banks[h, m, n][:], SILU, bias=b_sb[:, m : m + 1])
            nc.vector.tensor_tensor(
                windows[m][:].indirect(offs_sb[:, h * HALF // 16 : (h + 1) * HALF // 16]),
                y[:],
                wgo_sb[:, h * HALF : (h + 1) * HALF],
                MULT,
            )

        load(0, 0)
        nc.vector.memset(tiny[:], 0.0)
        nc.vector.memset(ws_sb[:].bitcast(I32), 0)
        nc.scalar.activation(tiny[:, 0:1], tiny[:, 1:2], SILU)
        nc.scalar.dma_start(w0_sb[:].bitcast(I32), w_view[:, :, 0 : 2 * P].bitcast(I32))
        for q in range(4):
            nc.scalar.dma_start(ws_sb[32 * q : 32 * q + 4, :, :].bitcast(I32), w_scales[:, 4 * q : 4 * q + 4, :].rearrange("a q n -> q a n").bitcast(I32))
        with nc.allow_non_contiguous_dma(reason="512 bias values, one to a partition and block"):
            nc.scalar.dma_start(b_sb[:], b.rearrange("(m p) -> p m", p=P))
        for a in range(1, PASSES):
            load(0, a)
        nc.sync.dma_start(offs_sb[:], offs)
        nc.sync.dma_start(wgo_sb[:, 0:HALF], wgo[:, 0:HALF])
        nc.sync.dma_start(w1_sb[:].bitcast(I32), w_view[:, :, 2 * P : 2 * M].bitcast(I32))
        clear(nc.vector, 0, 0, 2048)
        for lo in range(0, T, 1024):
            clear(nc.gpsimd, 2, lo, lo + 1024)

        for a in range(PASSES):
            quantize(0, a)
            multiply(0, a, 0)
            if a == 0:
                clear(nc.vector, 0, 2048, 3072)
                clear(nc.vector, 0, 3072, 4096)
            elif a < 3:
                clear(nc.vector, 1, 2048 * (a - 1), 2048 * (a - 1) + 1024)
                clear(nc.vector, 1, 2048 * (a - 1) + 1024, 2048 * a)
        load(1, 0)
        load(1, 1)
        nc.sync.dma_start(wgo_sb[:, HALF:S], wgo[:, HALF:S])
        load(1, 2)
        load(1, 3)
        window = stage.tile([P, T], F32, name="window", tag="stage")
        windows.append(window)
        for lo in range(0, T, 512):
            clear(nc.gpsimd, 3, lo, lo + 512)
        for m in range(BLOCKS):
            if m > 0:
                for a in range(PASSES):
                    multiply(0, a, m)
            if m == BLOCKS - 1:
                quantize(1, m)
            place(0, m)
            if m < BLOCKS - 1:
                quantize(1, m)
        for m in range(BLOCKS):
            for a in range(PASSES):
                multiply(1, a, m)
            place(1, m)
            nc.sync.dma_start(out[P * m : P * (m + 1), :], windows[m][:])
